import numpy as np
import ml_dtypes


def mxq(x, axis, fmt="e4m3"):
    dtype, down = {"e4m3": (ml_dtypes.float8_e4m3fn, 7), "e5m2": (ml_dtypes.float8_e5m2, 14)}[fmt]
    v = np.moveaxis(np.asarray(x, np.float32).astype(ml_dtypes.bfloat16).astype(np.float64), axis, -1)
    blocks = v.reshape(v.shape[:-1] + (-1, 32))
    amax = np.abs(blocks).max(-1, keepdims=True)
    byte = np.maximum(np.where(amax > 0, np.frexp(amax)[1] - 1 + 127, 0) - down, 1)
    scale = np.exp2(byte - 127.0)
    codes = (blocks / scale).astype(np.float32).astype(dtype).astype(np.float64)
    return np.moveaxis((codes * scale).reshape(v.shape), -1, axis)


WIDE = False


def mx_kscale(k):
    if not WIDE:
        return np.ones(k)
    levels = np.array([10, -10, 5, -5, 0])
    if k % 512:
        return np.exp2(np.random.permutation(np.resize(levels, k // 32))).repeat(32)
    a = np.empty((k // 512, 16))
    for p in range(k // 512):
        a[p, :8] = np.random.permutation(np.resize(levels, 8))
        for g in range(8):
            far = levels[np.abs(levels - a[p, g]) >= 10]
            a[p, g + 8] = far[np.random.randint(len(far))]
    return np.exp2(a.ravel()).repeat(32)


def f64(x):
    return np.asarray(x).astype(np.float64)


def striped(idx):
    return np.tile(np.asarray(idx).reshape(-1, 16).T, (8, 1)).astype(np.uint16)


def unstriped(offs):
    return offs[:16].T.reshape(-1).astype(np.int64)


def striped8(idx):
    return np.asarray(idx).reshape(8, -1, 16).transpose(0, 2, 1).reshape(128, -1).astype(np.uint16)


def unstriped8(offs):
    return offs.reshape(8, 16, -1).transpose(0, 2, 1).reshape(8, -1).astype(np.int64)


def pick8(x, idx, run):
    r = np.arange(len(x))
    return x[r[:, None], idx[r % (8 * run) // run]]


E2M1 = np.array([0.0, 0.5, 1.0, 1.5, 2.0, 3.0, 4.0, 6.0, -0.0, -0.5, -1.0, -1.5, -2.0, -3.0, -4.0, -6.0])


def pack_weight(w, fmt):
    k, n = w.shape
    w = f64(np.asarray(w, np.float32).astype(ml_dtypes.bfloat16)).reshape(k // 32, 32, n)
    amax = np.abs(w).max(1)
    if fmt == "e4m3":
        byte = np.frexp(amax)[1] - 1 + 127 - 7
    else:
        mant, ex = np.frexp(amax / 6.0)
        byte = np.where(mant > 0.5, ex, ex - 1) + 127
    byte = np.clip(np.where(amax > 0, byte, 1), 1, 254)
    scaled = (w * np.exp2(127.0 - byte)[:, None, :]).reshape(k, n).astype(np.float32)
    by_word = np.ascontiguousarray(scaled.reshape(k // 512, 128, 4, n).transpose(0, 1, 3, 2))
    if fmt == "e4m3":
        words = by_word.astype(ml_dtypes.float8_e4m3fn).view(np.uint8)
    else:
        c = by_word.astype(ml_dtypes.float4_e2m1fn).view(np.uint8) & 0xF
        words = (c[..., 0::2] | (c[..., 1::2] << 4)).reshape(k // 512, 128, 2 * n)
    return np.ascontiguousarray(words), np.ascontiguousarray(byte.astype(np.uint8).reshape(k // 512, 16, n))


def unpack_weight(words, scales, fmt):
    g, _, n = scales.shape
    words = np.ascontiguousarray(words).reshape(g, 128, n, -1)
    if fmt == "e4m3":
        vals = words.view(ml_dtypes.float8_e4m3fn).astype(np.float64)
    else:
        nib = np.empty((g, 128, n, 4), np.uint8)
        nib[..., 0::2] = words & 0xF
        nib[..., 1::2] = words >> 4
        vals = E2M1[nib]
    vals = vals * np.repeat(np.exp2(scales.astype(np.float64) - 127.0), 8, axis=1)[..., None]
    return vals.transpose(0, 1, 3, 2).reshape(g * 512, n)


def sigmoid(v):
    return 1.0 / (1.0 + np.exp(-v))


K, R, F, T, J, U, M = 512, 128, 512, 2048, 512, 1024, 256


def setup_inputs():
    n = np.random.standard_normal
    idx = np.random.permutation(T)[:J]
    idx2 = np.random.permutation(U)[:J]
    idx3 = np.stack([np.random.permutation(J)[:M] for _ in range(8)])
    fk = mx_kscale(K)
    dtabp = pack_weight(n((K, T)) / fk[:, None], "e2m1")
    tabp = pack_weight(n((K, T)) / fk[:, None], "e2m1")
    return {
        "dtab_words": dtabp[0],
        "dtab_scales": dtabp[1],
        "tab_words": tabp[0],
        "tab_scales": tabp[1],
        "w1": (n((K, R)) * 1 / np.sqrt(K) * fk[:, None]).astype(np.float32),
        "lift": (n((R, U)) * 0.5).astype(np.float32),
        "og": (np.random.uniform(0.5, 2.0, (R, 1))).astype(np.float32),
        "base": (0.3 * n((R, M))).astype(np.float32),
        "offs": striped(idx),
        "offs2": striped(idx2),
        "offs3": striped8(idx3),
    }


def reference(dtab_words, dtab_scales, tab_words, tab_scales, w1, lift, og, base, offs, offs2, offs3):
    idx = unstriped(offs)
    idx2 = unstriped(offs2)
    idx3 = unstriped8(offs3)
    dtabu = unpack_weight(dtab_words, dtab_scales, "e2m1")
    tabu = unpack_weight(tab_words, tab_scales, "e2m1")
    w1q = mxq(f64(w1), 0, "e4m3")
    tabidxg = tabu[:, idx]
    a = w1q.T @ tabidxg
    dtabidxg = dtabu[:, idx]
    ta = w1q.T @ dtabidxg
    h1 = np.tanh(a)
    h2 = h1 * np.exp(f64(lift)[:, idx2])
    th1 = ta * (1.0 - np.square(h1))
    th2 = th1 * np.exp(f64(lift)[:, idx2])
    tu1 = pick8(th2, idx3, 16) * sigmoid(pick8(h2, idx3, 16)) * (1.0 + pick8(h2, idx3, 16) * (1.0 - sigmoid(pick8(h2, idx3, 16))))
    y = tu1 * f64(og) + f64(base)
    return y

@@ -1,0 +1,111 @@
+from contextlib import ExitStack
+
+import concourse.mybir as mybir
+
+K, R, T, J, U, M = 512, 128, 2048, 512, 1024, 256
+FLOPS = 2 * 2 * K * R * J
+
+F32 = mybir.dt.float32
+BF16 = mybir.dt.bfloat16
+I32 = mybir.dt.int32
+U32 = mybir.dt.uint32
+U16 = mybir.dt.uint16
+U8 = mybir.dt.uint8
+FP8X4 = mybir.dt.float8_e4m3fn_x4
+FP4X4 = mybir.dt.float4_e2m1fn_x4
+ACT = mybir.ActivationFunctionType
+ALU = mybir.AluOpType
+
+P = 128
+PACK = 4
+
+
+def tile_attend_tliftedpicks_kernel(tc, dtab_words, dtab_scales, tab_words, tab_scales, w1, lift, og, base, offs, offs2, offs3, out):
+    nc = tc.nc
+    with ExitStack() as ctx:
+        sb = ctx.enter_context(tc.tile_pool(name="sb", bufs=1))
+        ps = ctx.enter_context(tc.psum_pool(name="ps", bufs=1))
+
+        cols = sb.tile([P, J // 16], U16, name="cols")
+        lifts = sb.tile([P, J // 16], U16, name="lifts")
+        picks = sb.tile([P, M // 16], U16, name="picks")
+        tw = sb.tile([P, T], U16, name="tw")
+        dw = sb.tile([P, T], U16, name="dw")
+        ts = sb.tile([P, T], U8, name="ts")
+        ds = sb.tile([P, T], U8, name="ds")
+        w_raw = sb.tile([P, PACK, R], F32, name="w_raw")
+        lift_sb = sb.tile([P, 2 * U], F32, name="lift_sb")
+        og_sb = sb.tile([P, 1], F32, name="og_sb")
+        base_sb = sb.tile([P, M], F32, name="base_sb")
+
+        nc.vector.memset(ts[:].bitcast(I32), 0)
+        nc.vector.memset(ds[:].bitcast(I32), 0)
+
+        def load_scales(queue, plane, rows):
+            for q in range(4):
+                queue.dma_start(out=plane[:].bitcast(I32)[32 * q : 32 * q + 4, :], in_=rows[0].bitcast(I32)[4 * q : 4 * q + 4, :])
+
+        nc.gpsimd.memset(lift_sb[:, U:], 0.0)
+        nc.sync.dma_start(cols[:], offs)
+        load_scales(nc.scalar, ts, tab_scales)
+        nc.sync.dma_start(out=tw[:].bitcast(I32), in_=tab_words[0].bitcast(I32))
+        nc.sync.dma_start(out=w_raw[:], in_=w1.rearrange("(p t) r -> p t r", t=PACK))
+        nc.sync.dma_start(lifts[:], offs2)
+        load_scales(nc.sync, ds, dtab_scales)
+        nc.sync.dma_start(out=lift_sb[:, :U], in_=lift)
+        nc.sync.dma_start(out=dw[:].bitcast(I32), in_=dtab_words[0].bitcast(I32))
+        nc.sync.dma_start(picks[:], offs3)
+        nc.gpsimd.dma_start(out=og_sb[:], in_=og)
+        nc.gpsimd.dma_start(out=base_sb[:], in_=base)
+
+        w_bf = sb.tile([P, R, PACK], BF16, name="w_bf", align_bytes=64)
+        nc.scalar.copy(out=w_bf[:], in_=w_raw[:].rearrange("p t r -> p r t"))
+        w_codes = sb.tile([P, R], U32, name="w_codes", align_bytes=64)
+        w_scales = sb.tile([P, R], U8, name="w_scales", align_bytes=64)
+
+        tsg = sb.tile([P, J], U8, name="tsg", align_bytes=64)
+        twg = sb.tile([P, J], U16, name="twg", align_bytes=64)
+        dsg = sb.tile([P, J], U8, name="dsg", align_bytes=64)
+        dwg = sb.tile([P, J], U16, name="dwg", align_bytes=64)
+        nc.vector.tensor_copy(tsg[:], ts[:].indirect(cols[:]))
+        nc.vector.quantize_mx(out=w_codes[:].bitcast(FP8X4), scales=w_scales[:], in_=w_bf[:].rearrange("p r t -> p (r t)"))
+        nc.vector.tensor_copy(twg[:], tw[:].indirect(cols[:]))
+        a = ps.tile([P, J], F32, name="a")
+        nc.tensor.matmul_mx(out=a[:], lhsT=w_codes[:].bitcast(FP8X4), lhsT_scale=w_scales[:], rhs=twg[:].bitcast(FP4X4), rhs_scale=tsg[:], start=True, stop=True)
+        nc.vector.tensor_copy(dsg[:], ds[:].indirect(cols[:]))
+        nc.vector.tensor_copy(dwg[:], dw[:].indirect(cols[:]))
+        ta = ps.tile([P, J], F32, name="ta")
+        nc.tensor.matmul_mx(out=ta[:], lhsT=w_codes[:].bitcast(FP8X4), lhsT_scale=w_scales[:], rhs=dwg[:].bitcast(FP4X4), rhs_scale=dsg[:], start=True, stop=True)
+
+        e = sb.tile([P, J], F32, name="e")
+        nc.scalar.activation(e[:], lift_sb[:].indirect(lifts[:]), ACT.Exp)
+        h1 = sb.tile([P, J], F32, name="h1")
+        nc.scalar.activation(h1[:], a[:], ACT.Tanh)
+        sq = sb.tile([P, J], F32, name="sq")
+        nc.scalar.activation(sq[:], h1[:], ACT.Square)
+        ogq = sb.tile([P, 1], F32, name="ogq")
+        nc.scalar.mul(ogq[:], og_sb[:], -0.25)
+
+        h2 = sb.tile([P, J], F32, name="h2")
+        nc.vector.tensor_tensor(h2[:], h1[:], e[:], ALU.mult)
+        nq = sb.tile([P, J], F32, name="nq")
+        nc.vector.scalar_tensor_tensor(nq[:], sq[:], 1.0, e[:], ALU.subtract, ALU.mult)
+        x = sb.tile([P, M], F32, name="x")
+        nc.vector.tensor_copy(x[:], h2[:].indirect(picks[:]))
+        th2 = sb.tile([P, J], F32, name="th2")
+        nc.vector.scalar_tensor_tensor(th2[:], ta[:], -1.0, nq[:], ALU.mult, ALU.mult)
+        tau = sb.tile([P, M], F32, name="tau")
+        nc.scalar.activation(tau[:], x[:], ACT.Tanh, scale=0.5)
+        g = sb.tile([P, M], F32, name="g")
+        nc.scalar.activation(g[:], tau[:], ACT.Identity, bias=ogq[:], scale=ogq[:])
+        c = sb.tile([P, M], F32, name="c")
+        nc.vector.scalar_tensor_tensor(c[:], tau[:], 1.0, x[:], ALU.subtract, ALU.mult)
+        t = sb.tile([P, M], F32, name="t")
+        nc.vector.tensor_copy(t[:], th2[:].indirect(picks[:]))
+        d = sb.tile([P, M], F32, name="d")
+        nc.vector.scalar_tensor_tensor(d[:], c[:], 2.0, g[:], ALU.subtract, ALU.mult)
+        y = sb.tile([P, M], F32, name="y")
+        nc.vector.tensor_tensor(y[:], t[:], d[:], ALU.mult)
+        res = sb.tile([P, M], F32, name="res")
+        nc.vector.tensor_tensor(res[:], y[:], base_sb[:], ALU.add)
+        nc.sync.dma_start(out=out, in_=res[:])

@@ -24,13 +24,14 @@ def tile_attend_tliftedpicks_kernel(tc, dtab_words, dtab_scales, tab_words, tab_
     nc = tc.nc
     with ExitStack() as ctx:
         sb = ctx.enter_context(tc.tile_pool(name="sb", bufs=1))
+        reuse = ctx.enter_context(tc.tile_pool(name="reuse", bufs=1))
         ps = ctx.enter_context(tc.psum_pool(name="ps", bufs=1))
 
         cols = sb.tile([P, J // 16], U16, name="cols")
         lifts = sb.tile([P, J // 16], U16, name="lifts")
         picks = sb.tile([P, M // 16], U16, name="picks")
         tw = sb.tile([P, T], U16, name="tw")
-        dw = sb.tile([P, T], U16, name="dw")
+        dw = reuse.tile([P, T], U16, name="dw", offset=0)
         ts = sb.tile([P, T], U8, name="ts")
         ds = sb.tile([P, T], U8, name="ds")
         w_raw = sb.tile([P, PACK, R], F32, name="w_raw")
@@ -38,25 +39,26 @@ def tile_attend_tliftedpicks_kernel(tc, dtab_words, dtab_scales, tab_words, tab_
         og_sb = sb.tile([P, 1], F32, name="og_sb")
         base_sb = sb.tile([P, M], F32, name="base_sb")
 
-        nc.vector.memset(ts[:].bitcast(I32), 0)
-        nc.vector.memset(ds[:].bitcast(I32), 0)
+        nc.gpsimd.memset(ts[:].bitcast(I32), 0)
+        nc.gpsimd.memset(ds[:].bitcast(I32), 0)
 
-        def load_scales(queue, plane, rows):
-            for q in range(4):
-                queue.dma_start(out=plane[:].bitcast(I32)[32 * q : 32 * q + 4, :], in_=rows[0].bitcast(I32)[4 * q : 4 * q + 4, :])
+        def load_scales(queue, plane, rows, q):
+            queue.dma_start(out=plane[:].bitcast(I32)[q : P : 32, :], in_=rows[0].bitcast(I32)[q : 16 : 4, :])
 
         nc.gpsimd.memset(lift_sb[:, U:], 0.0)
         nc.sync.dma_start(cols[:], offs)
-        load_scales(nc.scalar, ts, tab_scales)
         nc.sync.dma_start(out=tw[:].bitcast(I32), in_=tab_words[0].bitcast(I32))
+        for q in range(4):
+            load_scales(nc.sync, ts, tab_scales, q)
         nc.sync.dma_start(out=w_raw[:], in_=w1.rearrange("(p t) r -> p t r", t=PACK))
-        nc.sync.dma_start(lifts[:], offs2)
-        load_scales(nc.sync, ds, dtab_scales)
         nc.sync.dma_start(out=lift_sb[:, :U], in_=lift)
+        nc.sync.dma_start(lifts[:], offs2)
+        for q in range(4):
+            load_scales(nc.sync, ds, dtab_scales, q)
         nc.sync.dma_start(out=dw[:].bitcast(I32), in_=dtab_words[0].bitcast(I32))
         nc.sync.dma_start(picks[:], offs3)
-        nc.gpsimd.dma_start(out=og_sb[:], in_=og)
-        nc.gpsimd.dma_start(out=base_sb[:], in_=base)
+        nc.sync.dma_start(out=base_sb[:], in_=base)
+        nc.sync.dma_start(out=og_sb[:], in_=og)
 
         w_bf = sb.tile([P, R, PACK], BF16, name="w_bf", align_bytes=64)
         nc.scalar.copy(out=w_bf[:], in_=w_raw[:].rearrange("p t r -> p r t"))
@@ -67,9 +69,9 @@ def tile_attend_tliftedpicks_kernel(tc, dtab_words, dtab_scales, tab_words, tab_
         twg = sb.tile([P, J], U16, name="twg", align_bytes=64)
         dsg = sb.tile([P, J], U8, name="dsg", align_bytes=64)
         dwg = sb.tile([P, J], U16, name="dwg", align_bytes=64)
+        nc.vector.tensor_copy(twg[:], tw[:].indirect(cols[:]))
         nc.vector.tensor_copy(tsg[:], ts[:].indirect(cols[:]))
         nc.vector.quantize_mx(out=w_codes[:].bitcast(FP8X4), scales=w_scales[:], in_=w_bf[:].rearrange("p r t -> p (r t)"))
-        nc.vector.tensor_copy(twg[:], tw[:].indirect(cols[:]))
         a = ps.tile([P, J], F32, name="a")
         nc.tensor.matmul_mx(out=a[:], lhsT=w_codes[:].bitcast(FP8X4), lhsT_scale=w_scales[:], rhs=twg[:].bitcast(FP4X4), rhs_scale=tsg[:], start=True, stop=True)
         nc.vector.tensor_copy(dsg[:], ds[:].indirect(cols[:]))
@@ -86,26 +88,30 @@ def tile_attend_tliftedpicks_kernel(tc, dtab_words, dtab_scales, tab_words, tab_
         ogq = sb.tile([P, 1], F32, name="ogq")
         nc.scalar.mul(ogq[:], og_sb[:], -0.25)
 
-        h2 = sb.tile([P, J], F32, name="h2")
+        h2 = reuse.tile([P, J], F32, name="h2", offset=0)
         nc.vector.tensor_tensor(h2[:], h1[:], e[:], ALU.mult)
-        nq = sb.tile([P, J], F32, name="nq")
+        nq = reuse.tile([P, J], F32, name="nq", offset=4 * J)
         nc.vector.scalar_tensor_tensor(nq[:], sq[:], 1.0, e[:], ALU.subtract, ALU.mult)
         x = sb.tile([P, M], F32, name="x")
-        nc.vector.tensor_copy(x[:], h2[:].indirect(picks[:]))
         th2 = sb.tile([P, J], F32, name="th2")
-        nc.vector.scalar_tensor_tensor(th2[:], ta[:], -1.0, nq[:], ALU.mult, ALU.mult)
         tau = sb.tile([P, M], F32, name="tau")
-        nc.scalar.activation(tau[:], x[:], ACT.Tanh, scale=0.5)
         g = sb.tile([P, M], F32, name="g")
-        nc.scalar.activation(g[:], tau[:], ACT.Identity, bias=ogq[:], scale=ogq[:])
         c = sb.tile([P, M], F32, name="c")
-        nc.vector.scalar_tensor_tensor(c[:], tau[:], 1.0, x[:], ALU.subtract, ALU.mult)
-        t = sb.tile([P, M], F32, name="t")
-        nc.vector.tensor_copy(t[:], th2[:].indirect(picks[:]))
         d = sb.tile([P, M], F32, name="d")
-        nc.vector.scalar_tensor_tensor(d[:], c[:], 2.0, g[:], ALU.subtract, ALU.mult)
         y = sb.tile([P, M], F32, name="y")
-        nc.vector.tensor_tensor(y[:], t[:], d[:], ALU.mult)
         res = sb.tile([P, M], F32, name="res")
-        nc.vector.tensor_tensor(res[:], y[:], base_sb[:], ALU.add)
-        nc.sync.dma_start(out=out, in_=res[:])
+        halves = [slice(0, M // 2), slice(M // 2, M)]
+        half_picks = [picks[:, : M // 32], picks[:, M // 32 :]]
+        nc.vector.tensor_copy(x[:], h2[:].indirect(picks[:]))
+        nc.vector.scalar_tensor_tensor(th2[:], ta[:], -1.0, nq[:], ALU.mult, ALU.mult)
+        nc.scalar.activation(tau[:], x[:], ACT.Tanh, scale=0.5)
+        nc.scalar.activation(g[:], tau[:], ACT.Identity, bias=ogq[:], scale=ogq[:])
+        for s in halves:
+            nc.vector.scalar_tensor_tensor(c[:, s], tau[:, s], 1.0, x[:, s], ALU.subtract, ALU.mult)
+        for s in halves:
+            nc.vector.scalar_tensor_tensor(d[:, s], c[:, s], 2.0, g[:, s], ALU.subtract, ALU.mult)
+        for s, offsets in zip(halves, half_picks):
+            nc.vector.tensor_tensor(y[:, s], th2[:].indirect(offsets), d[:, s], ALU.mult)
+        for s in halves:
+            nc.vector.tensor_tensor(res[:, s], y[:, s], base_sb[:, s], ALU.add)
+            nc.sync.dma_start(out=out[:, s], in_=res[:, s])

@@ -31,34 +31,31 @@ def tile_attend_tliftedpicks_kernel(tc, dtab_words, dtab_scales, tab_words, tab_
         lifts = sb.tile([P, J // 16], U16, name="lifts")
         picks = sb.tile([P, M // 16], U16, name="picks")
         tw = sb.tile([P, T], U16, name="tw")
-        dw = reuse.tile([P, T], U16, name="dw", offset=0)
+        dw = sb.tile([P, T], U16, name="dw")
         ts = sb.tile([P, T], U8, name="ts")
         ds = sb.tile([P, T], U8, name="ds")
         w_raw = sb.tile([P, PACK, R], F32, name="w_raw")
-        lift_sb = sb.tile([P, 2 * U], F32, name="lift_sb")
+        lift_sb = reuse.tile([P, 2 * U], F32, name="lift_sb", offset=0)
         og_sb = sb.tile([P, 1], F32, name="og_sb")
         base_sb = sb.tile([P, M], F32, name="base_sb")
 
-        nc.gpsimd.memset(ts[:].bitcast(I32), 0)
         nc.gpsimd.memset(ds[:].bitcast(I32), 0)
+        nc.gpsimd.memset(ts[:].bitcast(I32), 0)
 
         def load_scales(queue, plane, rows, q):
             queue.dma_start(out=plane[:].bitcast(I32)[q : P : 32, :], in_=rows[0].bitcast(I32)[q : 16 : 4, :])
 
         nc.gpsimd.memset(lift_sb[:, U:], 0.0)
         nc.sync.dma_start(cols[:], offs)
+        nc.sync.dma_start(out=w_raw[:], in_=w1.rearrange("(p t) r -> p t r", t=PACK))
+        nc.sync.dma_start(out=ds[:].bitcast(I32)[0:P:8, :], in_=dtab_scales[0].bitcast(I32))
         nc.sync.dma_start(out=tw[:].bitcast(I32), in_=tab_words[0].bitcast(I32))
         for q in range(4):
             load_scales(nc.sync, ts, tab_scales, q)
-        nc.sync.dma_start(out=w_raw[:], in_=w1.rearrange("(p t) r -> p t r", t=PACK))
-        nc.sync.dma_start(out=lift_sb[:, :U], in_=lift)
         nc.sync.dma_start(lifts[:], offs2)
-        for q in range(4):
-            load_scales(nc.sync, ds, dtab_scales, q)
+        nc.sync.dma_start(out=lift_sb[:, :U], in_=lift)
         nc.sync.dma_start(out=dw[:].bitcast(I32), in_=dtab_words[0].bitcast(I32))
         nc.sync.dma_start(picks[:], offs3)
-        nc.sync.dma_start(out=base_sb[:], in_=base)
-        nc.sync.dma_start(out=og_sb[:], in_=og)
 
         w_bf = sb.tile([P, R, PACK], BF16, name="w_bf", align_bytes=64)
         nc.scalar.copy(out=w_bf[:], in_=w_raw[:].rearrange("p t r -> p r t"))
@@ -69,28 +66,36 @@ def tile_attend_tliftedpicks_kernel(tc, dtab_words, dtab_scales, tab_words, tab_
         twg = sb.tile([P, J], U16, name="twg", align_bytes=64)
         dsg = sb.tile([P, J], U8, name="dsg", align_bytes=64)
         dwg = sb.tile([P, J], U16, name="dwg", align_bytes=64)
-        nc.vector.tensor_copy(twg[:], tw[:].indirect(cols[:]))
-        nc.vector.tensor_copy(tsg[:], ts[:].indirect(cols[:]))
-        nc.vector.quantize_mx(out=w_codes[:].bitcast(FP8X4), scales=w_scales[:], in_=w_bf[:].rearrange("p r t -> p (r t)"))
-        a = ps.tile([P, J], F32, name="a")
-        nc.tensor.matmul_mx(out=a[:], lhsT=w_codes[:].bitcast(FP8X4), lhsT_scale=w_scales[:], rhs=twg[:].bitcast(FP4X4), rhs_scale=tsg[:], start=True, stop=True)
         nc.vector.tensor_copy(dsg[:], ds[:].indirect(cols[:]))
+        dsp = sb.tile([P, J], U8, name="dsp", align_bytes=64)
+        for i in range(4):
+            nc.sync.dma_start(out=dsp[:].bitcast(I32)[i:P:32, :], in_=dsg[:].bitcast(I32)[8 * i : P : 32, :])
+        nc.sync.dma_start(out=og_sb[:], in_=og)
+        nc.sync.dma_start(out=base_sb[:], in_=base)
+        nc.vector.quantize_mx(out=w_codes[:].bitcast(FP8X4), scales=w_scales[:], in_=w_bf[:].rearrange("p r t -> p (r t)"))
+        nc.vector.tensor_copy(twg[:], tw[:].indirect(cols[:]))
+        a_parts = []
+        for part in range(2):
+            s = slice(part * J // 2, (part + 1) * J // 2)
+            nc.vector.tensor_copy(tsg[:, s], ts[:].indirect(cols[:, part * J // 32 : (part + 1) * J // 32]))
+            a = ps.tile([P, J // 2], F32, name=f"a{part}")
+            nc.tensor.matmul_mx(out=a[:], lhsT=w_codes[:].bitcast(FP8X4), lhsT_scale=w_scales[:], rhs=twg[:, s].bitcast(FP4X4), rhs_scale=tsg[:, s], start=True, stop=True)
+            a_parts.append((s, a))
         nc.vector.tensor_copy(dwg[:], dw[:].indirect(cols[:]))
         ta = ps.tile([P, J], F32, name="ta")
-        nc.tensor.matmul_mx(out=ta[:], lhsT=w_codes[:].bitcast(FP8X4), lhsT_scale=w_scales[:], rhs=dwg[:].bitcast(FP4X4), rhs_scale=dsg[:], start=True, stop=True)
+        nc.tensor.matmul_mx(out=ta[:], lhsT=w_codes[:].bitcast(FP8X4), lhsT_scale=w_scales[:], rhs=dwg[:].bitcast(FP4X4), rhs_scale=dsp[:], start=True, stop=True)
 
         e = sb.tile([P, J], F32, name="e")
         nc.scalar.activation(e[:], lift_sb[:].indirect(lifts[:]), ACT.Exp)
-        h1 = sb.tile([P, J], F32, name="h1")
-        nc.scalar.activation(h1[:], a[:], ACT.Tanh)
+        h1 = reuse.tile([P, J], F32, name="h1", offset=0)
+        for s, a in a_parts:
+            nc.scalar.activation(h1[:, s], a[:], ACT.Tanh)
         sq = sb.tile([P, J], F32, name="sq")
         nc.scalar.activation(sq[:], h1[:], ACT.Square)
-        ogq = sb.tile([P, 1], F32, name="ogq")
-        nc.scalar.mul(ogq[:], og_sb[:], -0.25)
 
-        h2 = reuse.tile([P, J], F32, name="h2", offset=0)
+        h2 = sb.tile([P, J], F32, name="h2")
         nc.vector.tensor_tensor(h2[:], h1[:], e[:], ALU.mult)
-        nq = reuse.tile([P, J], F32, name="nq", offset=4 * J)
+        nq = sb.tile([P, J], F32, name="nq")
         nc.vector.scalar_tensor_tensor(nq[:], sq[:], 1.0, e[:], ALU.subtract, ALU.mult)
         x = sb.tile([P, M], F32, name="x")
         th2 = sb.tile([P, J], F32, name="th2")
@@ -105,7 +110,7 @@ def tile_attend_tliftedpicks_kernel(tc, dtab_words, dtab_scales, tab_words, tab_
         nc.vector.tensor_copy(x[:], h2[:].indirect(picks[:]))
         nc.vector.scalar_tensor_tensor(th2[:], ta[:], -1.0, nq[:], ALU.mult, ALU.mult)
         nc.scalar.activation(tau[:], x[:], ACT.Tanh, scale=0.5)
-        nc.scalar.activation(g[:], tau[:], ACT.Identity, bias=ogq[:], scale=ogq[:])
+        nc.scalar.activation(g[:], tau[:], ACT.Identity, bias=og_sb[:], scale=og_sb[:])
         for s in halves:
             nc.vector.scalar_tensor_tensor(c[:, s], tau[:, s], 1.0, x[:, s], ALU.subtract, ALU.mult)
         for s in halves:
@@ -113,5 +118,5 @@ def tile_attend_tliftedpicks_kernel(tc, dtab_words, dtab_scales, tab_words, tab_
         for s, offsets in zip(halves, half_picks):
             nc.vector.tensor_tensor(y[:, s], th2[:].indirect(offsets), d[:, s], ALU.mult)
         for s in halves:
-            nc.vector.tensor_tensor(res[:, s], y[:, s], base_sb[:, s], ALU.add)
+            nc.vector.scalar_tensor_tensor(res[:, s], y[:, s], -0.25, base_sb[:, s], ALU.mult, ALU.add)
             nc.sync.dma_start(out=out[:, s], in_=res[:, s])

@@ -18,105 +18,144 @@ ALU = mybir.AluOpType
 
 P = 128
 PACK = 4
+GROUP = 16
+QUADRANT = 32
+ROWS = 4
+BLOCK_PARTITIONS = 8
+MX_ALIGN = 64
+LIFT_WINDOW = 2 * U
+LIFT_BYTES = 4 * LIFT_WINDOW
 
 
-def tile_attend_tliftedpicks_kernel(tc, dtab_words, dtab_scales, tab_words, tab_scales, w1, lift, og, base, offs, offs2, offs3, out):
+def halves(n):
+    return slice(0, n // 2), slice(n // 2, n)
+
+
+def entries(offsets, s):
+    return offsets[:, s.start // GROUP : s.stop // GROUP]
+
+
+def tile_attend_tliftedpicks_kernel(
+    tc, dtab_words, dtab_scales, tab_words, tab_scales, w1, lift, og, base, offs, offs2, offs3, out
+):
     nc = tc.nc
     with ExitStack() as ctx:
         sb = ctx.enter_context(tc.tile_pool(name="sb", bufs=1))
         reuse = ctx.enter_context(tc.tile_pool(name="reuse", bufs=1))
         ps = ctx.enter_context(tc.psum_pool(name="ps", bufs=1))
 
-        cols = sb.tile([P, J // 16], U16, name="cols")
-        lifts = sb.tile([P, J // 16], U16, name="lifts")
-        picks = sb.tile([P, M // 16], U16, name="picks")
-        tw = sb.tile([P, T], U16, name="tw")
-        dw = sb.tile([P, T], U16, name="dw")
-        ts = sb.tile([P, T], U8, name="ts")
-        ds = sb.tile([P, T], U8, name="ds")
+        idx = sb.tile([P, J // GROUP], U16, name="idx")
+        idx2 = sb.tile([P, J // GROUP], U16, name="idx2")
+        idx3 = sb.tile([P, M // GROUP], U16, name="idx3")
+        tab_w = sb.tile([P, T], U16, name="tab_w")
+        dtab_w = sb.tile([P, T], U16, name="dtab_w")
+        tab_s = sb.tile([P, T], U8, name="tab_s")
+        dtab_s = sb.tile([P, T], U8, name="dtab_s")
         w_raw = sb.tile([P, PACK, R], F32, name="w_raw")
-        lift_sb = reuse.tile([P, 2 * U], F32, name="lift_sb", offset=0)
+        lift_sb = reuse.tile([P, LIFT_WINDOW], F32, name="lift_sb", offset=0)
         og_sb = sb.tile([P, 1], F32, name="og_sb")
         base_sb = sb.tile([P, M], F32, name="base_sb")
 
-        nc.gpsimd.memset(ds[:].bitcast(I32), 0)
-        nc.gpsimd.memset(ts[:].bitcast(I32), 0)
-
-        def load_scales(queue, plane, rows, q):
-            queue.dma_start(out=plane[:].bitcast(I32)[q : P : 32, :], in_=rows[0].bitcast(I32)[q : 16 : 4, :])
-
+        nc.gpsimd.memset(dtab_s[:].bitcast(I32), 0)
+        nc.gpsimd.memset(tab_s[:].bitcast(I32), 0)
         nc.gpsimd.memset(lift_sb[:, U:], 0.0)
-        nc.sync.dma_start(cols[:], offs)
+
+        nc.sync.dma_start(idx[:], offs)
         nc.sync.dma_start(out=w_raw[:], in_=w1.rearrange("(p t) r -> p t r", t=PACK))
-        nc.sync.dma_start(out=ds[:].bitcast(I32)[0:P:8, :], in_=dtab_scales[0].bitcast(I32))
-        nc.sync.dma_start(out=tw[:].bitcast(I32), in_=tab_words[0].bitcast(I32))
-        for q in range(4):
-            load_scales(nc.sync, ts, tab_scales, q)
-        nc.sync.dma_start(lifts[:], offs2)
+        nc.sync.dma_start(out=dtab_s[:].bitcast(I32)[0:P:BLOCK_PARTITIONS, :], in_=dtab_scales[0].bitcast(I32))
+        nc.sync.dma_start(out=tab_w[:].bitcast(I32), in_=tab_words[0].bitcast(I32))
+        for i in range(ROWS):
+            nc.sync.dma_start(
+                out=tab_s[:].bitcast(I32)[i:P:QUADRANT, :],
+                in_=tab_scales[0].bitcast(I32)[i : K // 32 : ROWS, :],
+            )
+        nc.sync.dma_start(idx2[:], offs2)
         nc.sync.dma_start(out=lift_sb[:, :U], in_=lift)
-        nc.sync.dma_start(out=dw[:].bitcast(I32), in_=dtab_words[0].bitcast(I32))
-        nc.sync.dma_start(picks[:], offs3)
+        nc.sync.dma_start(out=dtab_w[:].bitcast(I32), in_=dtab_words[0].bitcast(I32))
+        nc.sync.dma_start(idx3[:], offs3)
 
-        w_bf = sb.tile([P, R, PACK], BF16, name="w_bf", align_bytes=64)
+        w_bf = sb.tile([P, R, PACK], BF16, name="w_bf", align_bytes=MX_ALIGN)
         nc.scalar.copy(out=w_bf[:], in_=w_raw[:].rearrange("p t r -> p r t"))
-        w_codes = sb.tile([P, R], U32, name="w_codes", align_bytes=64)
-        w_scales = sb.tile([P, R], U8, name="w_scales", align_bytes=64)
+        w_codes = sb.tile([P, R], U32, name="w_codes", align_bytes=MX_ALIGN)
+        w_plane = sb.tile([P, R], U8, name="w_plane", align_bytes=MX_ALIGN)
 
-        tsg = sb.tile([P, J], U8, name="tsg", align_bytes=64)
-        twg = sb.tile([P, J], U16, name="twg", align_bytes=64)
-        dsg = sb.tile([P, J], U8, name="dsg", align_bytes=64)
-        dwg = sb.tile([P, J], U16, name="dwg", align_bytes=64)
-        nc.vector.tensor_copy(dsg[:], ds[:].indirect(cols[:]))
-        dsp = sb.tile([P, J], U8, name="dsp", align_bytes=64)
-        for i in range(4):
-            nc.sync.dma_start(out=dsp[:].bitcast(I32)[i:P:32, :], in_=dsg[:].bitcast(I32)[8 * i : P : 32, :])
+        tab_plane = sb.tile([P, J], U8, name="tab_plane", align_bytes=MX_ALIGN)
+        tab_codes = sb.tile([P, J], U16, name="tab_codes", align_bytes=MX_ALIGN)
+        dtab_rows = sb.tile([P, J], U8, name="dtab_rows", align_bytes=MX_ALIGN)
+        dtab_codes = sb.tile([P, J], U16, name="dtab_codes", align_bytes=MX_ALIGN)
+
+        nc.vector.tensor_copy(dtab_rows[:], dtab_s[:].indirect(idx[:]))
+        dtab_plane = sb.tile([P, J], U8, name="dtab_plane", align_bytes=MX_ALIGN)
+        for i in range(ROWS):
+            nc.sync.dma_start(
+                out=dtab_plane[:].bitcast(I32)[i:P:QUADRANT, :],
+                in_=dtab_rows[:].bitcast(I32)[BLOCK_PARTITIONS * i : P : QUADRANT, :],
+            )
         nc.sync.dma_start(out=og_sb[:], in_=og)
         nc.sync.dma_start(out=base_sb[:], in_=base)
-        nc.vector.quantize_mx(out=w_codes[:].bitcast(FP8X4), scales=w_scales[:], in_=w_bf[:].rearrange("p r t -> p (r t)"))
-        nc.vector.tensor_copy(twg[:], tw[:].indirect(cols[:]))
-        a_parts = []
-        for part in range(2):
-            s = slice(part * J // 2, (part + 1) * J // 2)
-            nc.vector.tensor_copy(tsg[:, s], ts[:].indirect(cols[:, part * J // 32 : (part + 1) * J // 32]))
+
+        nc.vector.quantize_mx(
+            out=w_codes[:].bitcast(FP8X4), scales=w_plane[:], in_=w_bf[:].rearrange("p r t -> p (r t)")
+        )
+
+        def product(acc, codes, plane):
+            nc.tensor.matmul_mx(
+                out=acc,
+                lhsT=w_codes[:].bitcast(FP8X4),
+                lhsT_scale=w_plane[:],
+                rhs=codes.bitcast(FP4X4),
+                rhs_scale=plane,
+                start=True,
+                stop=True,
+            )
+
+        nc.vector.tensor_copy(tab_codes[:], tab_w[:].indirect(idx[:]))
+        a_halves = []
+        for part, s in enumerate(halves(J)):
+            nc.vector.tensor_copy(tab_plane[:, s], tab_s[:].indirect(entries(idx, s)))
             a = ps.tile([P, J // 2], F32, name=f"a{part}")
-            nc.tensor.matmul_mx(out=a[:], lhsT=w_codes[:].bitcast(FP8X4), lhsT_scale=w_scales[:], rhs=twg[:, s].bitcast(FP4X4), rhs_scale=tsg[:, s], start=True, stop=True)
-            a_parts.append((s, a))
-        nc.vector.tensor_copy(dwg[:], dw[:].indirect(cols[:]))
+            product(a[:], tab_codes[:, s], tab_plane[:, s])
+            a_halves.append(a)
+        nc.vector.tensor_copy(dtab_codes[:], dtab_w[:].indirect(idx[:]))
         ta = ps.tile([P, J], F32, name="ta")
-        nc.tensor.matmul_mx(out=ta[:], lhsT=w_codes[:].bitcast(FP8X4), lhsT_scale=w_scales[:], rhs=dwg[:].bitcast(FP4X4), rhs_scale=dsp[:], start=True, stop=True)
+        product(ta[:], dtab_codes[:], dtab_plane[:])
 
         e = sb.tile([P, J], F32, name="e")
-        nc.scalar.activation(e[:], lift_sb[:].indirect(lifts[:]), ACT.Exp)
+        nc.scalar.activation(e[:], lift_sb[:].indirect(idx2[:]), ACT.Exp)
         h1 = reuse.tile([P, J], F32, name="h1", offset=0)
-        for s, a in a_parts:
+        for s, a in zip(halves(J), a_halves):
             nc.scalar.activation(h1[:, s], a[:], ACT.Tanh)
-        sq = sb.tile([P, J], F32, name="sq")
-        nc.scalar.activation(sq[:], h1[:], ACT.Square)
+        h1_sq = sb.tile([P, J], F32, name="h1_sq")
+        for s in halves(J):
+            nc.scalar.activation(h1_sq[:, s], h1[:, s], ACT.Square)
 
+        first, second = halves(J)
         h2 = sb.tile([P, J], F32, name="h2")
         nc.vector.tensor_tensor(h2[:], h1[:], e[:], ALU.mult)
-        nq = sb.tile([P, J], F32, name="nq")
-        nc.vector.scalar_tensor_tensor(nq[:], sq[:], 1.0, e[:], ALU.subtract, ALU.mult)
+        slope0 = reuse.tile([P, J // 2], F32, name="slope0", offset=LIFT_BYTES)
+        slope1 = sb.tile([P, J // 2], F32, name="slope1")
+        nc.vector.scalar_tensor_tensor(slope0[:], h1_sq[:, first], 1.0, e[:, first], ALU.subtract, ALU.mult)
         x = sb.tile([P, M], F32, name="x")
         th2 = sb.tile([P, J], F32, name="th2")
         tau = sb.tile([P, M], F32, name="tau")
-        g = sb.tile([P, M], F32, name="g")
-        c = sb.tile([P, M], F32, name="c")
-        d = sb.tile([P, M], F32, name="d")
+        gain = sb.tile([P, M], F32, name="gain")
+        bend = reuse.tile([P, M], F32, name="bend", offset=LIFT_BYTES)
+        factor = sb.tile([P, M], F32, name="factor")
         y = sb.tile([P, M], F32, name="y")
         res = sb.tile([P, M], F32, name="res")
-        halves = [slice(0, M // 2), slice(M // 2, M)]
-        half_picks = [picks[:, : M // 32], picks[:, M // 32 :]]
-        nc.vector.tensor_copy(x[:], h2[:].indirect(picks[:]))
-        nc.vector.scalar_tensor_tensor(th2[:], ta[:], -1.0, nq[:], ALU.mult, ALU.mult)
+        nc.vector.tensor_copy(x[:], h2[:].indirect(idx3[:]))
+        nc.vector.scalar_tensor_tensor(slope1[:], h1_sq[:, second], 1.0, e[:, second], ALU.subtract, ALU.mult)
+        nc.vector.scalar_tensor_tensor(th2[:, first], ta[:, first], -1.0, slope0[:], ALU.mult, ALU.mult)
+        nc.vector.scalar_tensor_tensor(th2[:, second], ta[:, second], -1.0, slope1[:], ALU.mult, ALU.mult)
+
         nc.scalar.activation(tau[:], x[:], ACT.Tanh, scale=0.5)
-        nc.scalar.activation(g[:], tau[:], ACT.Identity, bias=og_sb[:], scale=og_sb[:])
-        for s in halves:
-            nc.vector.scalar_tensor_tensor(c[:, s], tau[:, s], 1.0, x[:, s], ALU.subtract, ALU.mult)
-        for s in halves:
-            nc.vector.scalar_tensor_tensor(d[:, s], c[:, s], 2.0, g[:, s], ALU.subtract, ALU.mult)
-        for s, offsets in zip(halves, half_picks):
-            nc.vector.tensor_tensor(y[:, s], th2[:].indirect(offsets), d[:, s], ALU.mult)
-        for s in halves:
+        nc.scalar.activation(gain[:], tau[:], ACT.Identity, bias=og_sb[:], scale=og_sb[:])
+        for s in halves(M):
+            nc.vector.scalar_tensor_tensor(bend[:, s], tau[:, s], 1.0, x[:, s], ALU.subtract, ALU.mult)
+        for s in halves(M):
+            nc.vector.scalar_tensor_tensor(factor[:, s], bend[:, s], 2.0, gain[:, s], ALU.subtract, ALU.mult)
+        for s in halves(M):
+            nc.vector.tensor_tensor(y[:, s], th2[:].indirect(entries(idx3, s)), factor[:, s], ALU.mult)
+        for s in halves(M):
             nc.vector.scalar_tensor_tensor(res[:, s], y[:, s], -0.25, base_sb[:, s], ALU.mult, ALU.add)
             nc.sync.dma_start(out=out[:, s], in_=res[:, s])

from contextlib import ExitStack

import concourse.mybir as mybir

K, R, T, J, U, M = 512, 128, 2048, 512, 1024, 256
FLOPS = 2 * 2 * K * R * J

F32 = mybir.dt.float32
BF16 = mybir.dt.bfloat16
I32 = mybir.dt.int32
U32 = mybir.dt.uint32
U16 = mybir.dt.uint16
U8 = mybir.dt.uint8
FP8X4 = mybir.dt.float8_e4m3fn_x4
FP4X4 = mybir.dt.float4_e2m1fn_x4
ACT = mybir.ActivationFunctionType
ALU = mybir.AluOpType

P = 128
PACK = 4
GROUP = 16
QUADRANT = 32
ROWS = 4
BLOCK_PARTITIONS = 8
MX_ALIGN = 64
LIFT_WINDOW = 2 * U
LIFT_BYTES = 4 * LIFT_WINDOW


def halves(n):
    return slice(0, n // 2), slice(n // 2, n)


def entries(offsets, s):
    return offsets[:, s.start // GROUP : s.stop // GROUP]


def tile_attend_tliftedpicks_kernel(
    tc, dtab_words, dtab_scales, tab_words, tab_scales, w1, lift, og, base, offs, offs2, offs3, out
):
    nc = tc.nc
    with ExitStack() as ctx:
        sb = ctx.enter_context(tc.tile_pool(name="sb", bufs=1))
        reuse = ctx.enter_context(tc.tile_pool(name="reuse", bufs=1))
        ps = ctx.enter_context(tc.psum_pool(name="ps", bufs=1))

        idx = sb.tile([P, J // GROUP], U16, name="idx")
        idx2 = sb.tile([P, J // GROUP], U16, name="idx2")
        idx3 = sb.tile([P, M // GROUP], U16, name="idx3")
        tab_w = sb.tile([P, T], U16, name="tab_w")
        dtab_w = sb.tile([P, T], U16, name="dtab_w")
        tab_s = sb.tile([P, T], U8, name="tab_s")
        dtab_s = sb.tile([P, T], U8, name="dtab_s")
        w_raw = sb.tile([P, PACK, R], F32, name="w_raw")
        lift_sb = reuse.tile([P, LIFT_WINDOW], F32, name="lift_sb", offset=0)
        og_sb = sb.tile([P, 1], F32, name="og_sb")
        base_sb = sb.tile([P, M], F32, name="base_sb")

        nc.gpsimd.memset(dtab_s[:].bitcast(I32), 0)
        nc.gpsimd.memset(tab_s[:].bitcast(I32), 0)
        nc.gpsimd.memset(lift_sb[:, U:], 0.0)

        nc.sync.dma_start(idx[:], offs)
        nc.sync.dma_start(out=w_raw[:], in_=w1.rearrange("(p t) r -> p t r", t=PACK))
        nc.sync.dma_start(out=dtab_s[:].bitcast(I32)[0:P:BLOCK_PARTITIONS, :], in_=dtab_scales[0].bitcast(I32))
        nc.sync.dma_start(out=tab_w[:].bitcast(I32), in_=tab_words[0].bitcast(I32))
        for i in range(ROWS):
            nc.sync.dma_start(
                out=tab_s[:].bitcast(I32)[i:P:QUADRANT, :],
                in_=tab_scales[0].bitcast(I32)[i : K // 32 : ROWS, :],
            )
        nc.sync.dma_start(idx2[:], offs2)
        nc.sync.dma_start(out=lift_sb[:, :U], in_=lift)
        nc.sync.dma_start(out=dtab_w[:].bitcast(I32), in_=dtab_words[0].bitcast(I32))
        nc.sync.dma_start(idx3[:], offs3)

        w_bf = sb.tile([P, R, PACK], BF16, name="w_bf", align_bytes=MX_ALIGN)
        nc.scalar.copy(out=w_bf[:], in_=w_raw[:].rearrange("p t r -> p r t"))
        w_codes = sb.tile([P, R], U32, name="w_codes", align_bytes=MX_ALIGN)
        w_plane = sb.tile([P, R], U8, name="w_plane", align_bytes=MX_ALIGN)

        tab_plane = sb.tile([P, J], U8, name="tab_plane", align_bytes=MX_ALIGN)
        tab_codes = sb.tile([P, J], U16, name="tab_codes", align_bytes=MX_ALIGN)
        dtab_rows = sb.tile([P, J], U8, name="dtab_rows", align_bytes=MX_ALIGN)
        dtab_codes = sb.tile([P, J], U16, name="dtab_codes", align_bytes=MX_ALIGN)

        nc.vector.tensor_copy(dtab_rows[:], dtab_s[:].indirect(idx[:]))
        dtab_plane = sb.tile([P, J], U8, name="dtab_plane", align_bytes=MX_ALIGN)
        for i in range(ROWS):
            nc.sync.dma_start(
                out=dtab_plane[:].bitcast(I32)[i:P:QUADRANT, :],
                in_=dtab_rows[:].bitcast(I32)[BLOCK_PARTITIONS * i : P : QUADRANT, :],
            )
        nc.sync.dma_start(out=og_sb[:], in_=og)
        nc.sync.dma_start(out=base_sb[:], in_=base)

        nc.vector.quantize_mx(
            out=w_codes[:].bitcast(FP8X4), scales=w_plane[:], in_=w_bf[:].rearrange("p r t -> p (r t)")
        )

        def product(acc, codes, plane):
            nc.tensor.matmul_mx(
                out=acc,
                lhsT=w_codes[:].bitcast(FP8X4),
                lhsT_scale=w_plane[:],
                rhs=codes.bitcast(FP4X4),
                rhs_scale=plane,
                start=True,
                stop=True,
            )

        nc.vector.tensor_copy(tab_codes[:], tab_w[:].indirect(idx[:]))
        a_halves = []
        for part, s in enumerate(halves(J)):
            nc.vector.tensor_copy(tab_plane[:, s], tab_s[:].indirect(entries(idx, s)))
            a = ps.tile([P, J // 2], F32, name=f"a{part}")
            product(a[:], tab_codes[:, s], tab_plane[:, s])
            a_halves.append(a)
        nc.vector.tensor_copy(dtab_codes[:], dtab_w[:].indirect(idx[:]))
        ta = ps.tile([P, J], F32, name="ta")
        product(ta[:], dtab_codes[:], dtab_plane[:])

        e = sb.tile([P, J], F32, name="e")
        nc.scalar.activation(e[:], lift_sb[:].indirect(idx2[:]), ACT.Exp)
        h1 = reuse.tile([P, J], F32, name="h1", offset=0)
        for s, a in zip(halves(J), a_halves):
            nc.scalar.activation(h1[:, s], a[:], ACT.Tanh)
        h1_sq = sb.tile([P, J], F32, name="h1_sq")
        for s in halves(J):
            nc.scalar.activation(h1_sq[:, s], h1[:, s], ACT.Square)

        first, second = halves(J)
        h2 = sb.tile([P, J], F32, name="h2")
        nc.vector.tensor_tensor(h2[:], h1[:], e[:], ALU.mult)
        slope0 = reuse.tile([P, J // 2], F32, name="slope0", offset=LIFT_BYTES)
        slope1 = sb.tile([P, J // 2], F32, name="slope1")
        nc.vector.scalar_tensor_tensor(slope0[:], h1_sq[:, first], 1.0, e[:, first], ALU.subtract, ALU.mult)
        x = sb.tile([P, M], F32, name="x")
        th2 = sb.tile([P, J], F32, name="th2")
        tau = sb.tile([P, M], F32, name="tau")
        gain = sb.tile([P, M], F32, name="gain")
        bend = reuse.tile([P, M], F32, name="bend", offset=LIFT_BYTES)
        factor = sb.tile([P, M], F32, name="factor")
        y = sb.tile([P, M], F32, name="y")
        res = sb.tile([P, M], F32, name="res")
        nc.vector.tensor_copy(x[:], h2[:].indirect(idx3[:]))
        nc.vector.scalar_tensor_tensor(slope1[:], h1_sq[:, second], 1.0, e[:, second], ALU.subtract, ALU.mult)
        nc.vector.scalar_tensor_tensor(th2[:, first], ta[:, first], -1.0, slope0[:], ALU.mult, ALU.mult)
        nc.vector.scalar_tensor_tensor(th2[:, second], ta[:, second], -1.0, slope1[:], ALU.mult, ALU.mult)

        nc.scalar.activation(tau[:], x[:], ACT.Tanh, scale=0.5)
        nc.scalar.activation(gain[:], tau[:], ACT.Identity, bias=og_sb[:], scale=og_sb[:])
        for s in halves(M):
            nc.vector.scalar_tensor_tensor(bend[:, s], tau[:, s], 1.0, x[:, s], ALU.subtract, ALU.mult)
        for s in halves(M):
            nc.vector.scalar_tensor_tensor(factor[:, s], bend[:, s], 2.0, gain[:, s], ALU.subtract, ALU.mult)
        for s in halves(M):
            nc.vector.tensor_tensor(y[:, s], th2[:].indirect(entries(idx3, s)), factor[:, s], ALU.mult)
        for s in halves(M):
            nc.vector.scalar_tensor_tensor(res[:, s], y[:, s], -0.25, base_sb[:, s], ALU.mult, ALU.add)
            nc.sync.dma_start(out=out[:, s], in_=res[:, s])
